import numpy as np
import ml_dtypes

BF16 = ml_dtypes.bfloat16


def bf(x):
    return np.asarray(x, np.float32).astype(BF16)


def f32(x):
    return np.asarray(x, np.float32)


def f64(x):
    return np.asarray(x).astype(np.float64)


def striped(idx):
    return np.tile(idx.reshape(-1, 16).T, (8, 1))


def rows(idx, k):
    return np.tile(idx, (k, 1))


def look(tab, idx):
    return np.take_along_axis(f64(tab), rows(idx, len(tab)), axis=1)


K, S, V, N, M = 512, 256, 256, 256, 512


def setup_inputs():
    return {"tab": f32(np.random.standard_normal((K, S))), "y": f32(np.random.standard_normal((K, V))), "w": bf(np.random.standard_normal((K, M)) / np.sqrt(K)), "b": f32(0.5 * np.random.standard_normal((M, 1))), "offs": striped(np.random.permutation(S)[:N])}


def reference(tab, y, w, b, offs):
    idx = offs[:16].T.reshape(-1)
    t = look(tab, idx)
    x = np.maximum(t, 0.0) * f64(y)
    y = f64(w).T @ x
    return np.maximum(y + f64(b), 0.0)

@@ -1,0 +1,62 @@
+import concourse.mybir as mybir
+
+F32, BF16, U16 = mybir.dt.float32, mybir.dt.bfloat16, mybir.dt.uint16
+MULT, ADD, MAX = mybir.AluOpType.mult, mybir.AluOpType.add, mybir.AluOpType.max
+RELU = mybir.ActivationFunctionType.Relu
+
+P = 128
+K, S, N, M = 512, 256, 256, 512
+KB, MB = K // P, M // P
+PIECE = 128
+STRIPE = 16
+
+FLOPS = 2 * K * M * N
+
+
+def tile_lookup_gate_relu_relu_kernel(tc, tab, y, w, b, offs, out):
+    nc = tc.nc
+    tab_rows = tab.rearrange("(p c) s -> p c s", c=KB)
+    out_rows = out.rearrange("(p c) j -> p c j", c=MB)
+
+    with (
+        tc.tile_pool(name="held", bufs=1) as held,
+        tc.tile_pool(name="work", bufs=4) as work,
+        tc.psum_pool(name="psum", bufs=1) as psum,
+    ):
+        offsets = held.tile([P, N // STRIPE], U16, name="offsets")
+        nc.sync.dma_start(offsets[:], offs)
+
+        windows = []
+        for k in range(KB):
+            window = held.tile([P, S], F32, name=f"window{k}")
+            nc.sync.dma_start(window[:], tab_rows[:, k, :])
+            windows.append(window)
+
+        stream = held.tile([P, KB, N], F32, name="stream")
+        nc.scalar.dma_start(stream[:], y.rearrange("(p c) j -> p c j", c=KB))
+        weights = held.tile([P, KB, M], BF16, name="weights")
+        nc.scalar.dma_start(weights[:], w.rearrange("(p c) m -> p c m", c=KB))
+        bias = held.tile([P, MB], F32, name="bias")
+        nc.gpsimd.dma_start(bias[:], b.rearrange("(p c) o -> p (c o)", c=MB))
+
+        sums = [psum.tile([P, N], F32, name=f"sum{m}") for m in range(MB)]
+
+        for k in range(KB):
+            gate = work.tile([P, N], F32, name="gate")
+            for j in range(0, N, PIECE):
+                entries = offsets[:, j // STRIPE : (j + PIECE) // STRIPE]
+                nc.scalar.activation(gate[:, j : j + PIECE], windows[k][:].indirect(entries), RELU)
+            x = work.tile([P, N], BF16, name="x")
+            nc.vector.tensor_tensor(x[:], gate[:], stream[:, k, :], MULT)
+            for m in range(MB):
+                nc.tensor.matmul(
+                    sums[m][:], weights[:, k, m::MB], x[:], start=(k == 0), stop=(k == KB - 1)
+                )
+
+        for m in range(MB):
+            row = work.tile([P, N], F32, name="row")
+            if m % 2 == 0:
+                nc.scalar.activation(row[:], sums[m][:], RELU, bias=bias[:, m : m + 1])
+            else:
+                nc.vector.tensor_scalar(row[:], sums[m][:], bias[:, m : m + 1], 0.0, ADD, MAX)
+            nc.sync.dma_start(out_rows[:, m, :], row[:])

@@ -9,13 +9,14 @@ K, S, N, M = 512, 256, 256, 512
 KB, MB = K // P, M // P
 PIECE = 128
 STRIPE = 16
-
 FLOPS = 2 * K * M * N
 
 
 def tile_lookup_gate_relu_relu_kernel(tc, tab, y, w, b, offs, out):
     nc = tc.nc
     tab_rows = tab.rearrange("(p c) s -> p c s", c=KB)
+    y_rows = y.rearrange("(p c) j -> p c j", c=KB)
+    w_rows = w.rearrange("(p c) m -> p c m", c=KB)
     out_rows = out.rearrange("(p c) j -> p c j", c=MB)
 
     with (
@@ -23,19 +24,23 @@ def tile_lookup_gate_relu_relu_kernel(tc, tab, y, w, b, offs, out):
         tc.tile_pool(name="work", bufs=4) as work,
         tc.psum_pool(name="psum", bufs=1) as psum,
     ):
+        zeros = held.tile([P, 1], F32, name="zeros")
+        nc.vector.memset(zeros[:], 0.0)
+        warm = held.tile([P, 1], F32, name="warm")
+        nc.scalar.activation(warm[:], zeros[:], RELU)
+
         offsets = held.tile([P, N // STRIPE], U16, name="offsets")
         nc.sync.dma_start(offsets[:], offs)
 
-        windows = []
+        windows = [held.tile([P, S], F32, name=f"window{k}") for k in range(KB)]
+        streams = [held.tile([P, N], F32, name=f"stream{k}") for k in range(KB)]
+        weights = [held.tile([P, M], BF16, name=f"weights{k}") for k in range(KB)]
+        nc.sync.dma_start(windows[0][:], tab_rows[:, 0, :])
         for k in range(KB):
-            window = held.tile([P, S], F32, name=f"window{k}")
-            nc.sync.dma_start(window[:], tab_rows[:, k, :])
-            windows.append(window)
-
-        stream = held.tile([P, KB, N], F32, name="stream")
-        nc.scalar.dma_start(stream[:], y.rearrange("(p c) j -> p c j", c=KB))
-        weights = held.tile([P, KB, M], BF16, name="weights")
-        nc.scalar.dma_start(weights[:], w.rearrange("(p c) m -> p c m", c=KB))
+            if k + 1 < KB:
+                nc.sync.dma_start(windows[k + 1][:], tab_rows[:, k + 1, :])
+            nc.sync.dma_start(streams[k][:], y_rows[:, k, :])
+            nc.sync.dma_start(weights[k][:], w_rows[:, k, :])
         bias = held.tile([P, MB], F32, name="bias")
         nc.gpsimd.dma_start(bias[:], b.rearrange("(p c) o -> p (c o)", c=MB))
 
@@ -47,10 +52,10 @@ def tile_lookup_gate_relu_relu_kernel(tc, tab, y, w, b, offs, out):
                 entries = offsets[:, j // STRIPE : (j + PIECE) // STRIPE]
                 nc.scalar.activation(gate[:, j : j + PIECE], windows[k][:].indirect(entries), RELU)
             x = work.tile([P, N], BF16, name="x")
-            nc.vector.tensor_tensor(x[:], gate[:], stream[:, k, :], MULT)
+            nc.vector.tensor_tensor(x[:], gate[:], streams[k][:], MULT)
             for m in range(MB):
                 nc.tensor.matmul(
-                    sums[m][:], weights[:, k, m::MB], x[:], start=(k == 0), stop=(k == KB - 1)
+                    sums[m][:], weights[k][:, m::MB], x[:], start=(k == 0), stop=(k == KB - 1)
                 )
 
         for m in range(MB):

import concourse.mybir as mybir

F32, BF16, U16 = mybir.dt.float32, mybir.dt.bfloat16, mybir.dt.uint16
MULT, ADD, MAX = mybir.AluOpType.mult, mybir.AluOpType.add, mybir.AluOpType.max
RELU = mybir.ActivationFunctionType.Relu

P = 128
K, S, N, M = 512, 256, 256, 512
KB, MB = K // P, M // P
PIECE = 128
STRIPE = 16
FLOPS = 2 * K * M * N


def tile_lookup_gate_relu_relu_kernel(tc, tab, y, w, b, offs, out):
    nc = tc.nc
    tab_rows = tab.rearrange("(p c) s -> p c s", c=KB)
    y_rows = y.rearrange("(p c) j -> p c j", c=KB)
    w_rows = w.rearrange("(p c) m -> p c m", c=KB)
    out_rows = out.rearrange("(p c) j -> p c j", c=MB)

    with (
        tc.tile_pool(name="held", bufs=1) as held,
        tc.tile_pool(name="work", bufs=4) as work,
        tc.psum_pool(name="psum", bufs=1) as psum,
    ):
        zeros = held.tile([P, 1], F32, name="zeros")
        nc.vector.memset(zeros[:], 0.0)
        warm = held.tile([P, 1], F32, name="warm")
        nc.scalar.activation(warm[:], zeros[:], RELU)

        offsets = held.tile([P, N // STRIPE], U16, name="offsets")
        nc.sync.dma_start(offsets[:], offs)

        windows = [held.tile([P, S], F32, name=f"window{k}") for k in range(KB)]
        streams = [held.tile([P, N], F32, name=f"stream{k}") for k in range(KB)]
        weights = [held.tile([P, M], BF16, name=f"weights{k}") for k in range(KB)]
        nc.sync.dma_start(windows[0][:], tab_rows[:, 0, :])
        for k in range(KB):
            if k + 1 < KB:
                nc.sync.dma_start(windows[k + 1][:], tab_rows[:, k + 1, :])
            nc.sync.dma_start(streams[k][:], y_rows[:, k, :])
            nc.sync.dma_start(weights[k][:], w_rows[:, k, :])
        bias = held.tile([P, MB], F32, name="bias")
        nc.gpsimd.dma_start(bias[:], b.rearrange("(p c) o -> p (c o)", c=MB))

        sums = [psum.tile([P, N], F32, name=f"sum{m}") for m in range(MB)]

        for k in range(KB):
            gate = work.tile([P, N], F32, name="gate")
            for j in range(0, N, PIECE):
                entries = offsets[:, j // STRIPE : (j + PIECE) // STRIPE]
                nc.scalar.activation(gate[:, j : j + PIECE], windows[k][:].indirect(entries), RELU)
            x = work.tile([P, N], BF16, name="x")
            nc.vector.tensor_tensor(x[:], gate[:], streams[k][:], MULT)
            for m in range(MB):
                nc.tensor.matmul(
                    sums[m][:], weights[k][:, m::MB], x[:], start=(k == 0), stop=(k == KB - 1)
                )

        for m in range(MB):
            row = work.tile([P, N], F32, name="row")
            if m % 2 == 0:
                nc.scalar.activation(row[:], sums[m][:], RELU, bias=bias[:, m : m + 1])
            else:
                nc.vector.tensor_scalar(row[:], sums[m][:], bias[:, m : m + 1], 0.0, ADD, MAX)
            nc.sync.dma_start(out_rows[:, m, :], row[:])
